import numpy as np, ml_dtypes
CORES = [12,28,60,100,156,228]
N = 6
import mx_ref
NC = 128
BF = ml_dtypes.bfloat16
def setup_inputs(rng):
    def f(*shape):
        return mx_ref.flush((rng.standard_normal(shape, dtype=np.float32) * np.exp2(rng.integers(-2, 3, shape[:-1] + (1,)))).astype(BF))
    return {"x": f(N, 128, 512), "rt": f(N, 128, 512), "w": f(N, 128, 4 * NC)}
def setup_inputs_blocks(rng):
    d = setup_inputs(rng)
    for k in ("x", "rt", "w"): d[k] = mx_ref.spread(d[k], rng, 1)
    return d
def setup_inputs_wide(rng):
    d = setup_inputs(rng)
    for k in ("x", "rt", "w"): d[k] = mx_ref.flush((d[k].astype(np.float32) * np.exp2(rng.integers(-6, 7, (N, 1, 1))).astype(np.float32)).astype(BF))
    return d
def setup_inputs_near(rng):
    d = setup_inputs(rng); v = d["rt"].astype(np.float32).reshape(N, 128, -1, 4)
    d["rt"] = mx_ref.flush((v[:, :, :1] + v / 64).reshape(d["rt"].shape).astype(BF))
    return d
def setup_inputs_twins(rng):
    d = setup_inputs(rng); v = d["rt"].reshape(N, 128, -1, 4).copy()
    v[:, :, 1] = v[:, :, 0]
    d["rt"] = v.reshape(d["rt"].shape)
    return d
def reference(x, rt, w):
    W = [mx_ref.quantize(w[e]) for e in range(N)]
    y = np.zeros((N, 128, NC), np.float32)
    for j in range(N):
        X = mx_ref.quantize(x[j])
        lg = mx_ref.matmul(X, mx_ref.quantize(rt[j]))[:, :N]
        m = lg.max(axis=1, keepdims=True); m2 = np.where(lg < m, lg, -np.inf).max(axis=1, keepdims=True)
        for e in range(N):
            y[j] = y[j] + (lg[:, e:e + 1] >= m2) * (mx_ref.matmul(X, W[e]) * lg[:, e:e + 1])
    return {"y": y}

from concourse.bass import DstId, RemoteDMATransfer
from concourse.mybir import dt, AluOpType, AxisListType, ActivationFunctionType

N = 6
NC = 128
BANK = 512
CORES_ALL = 256
BIG = 1.0e29

SCRATCH = {
    "xin": ("sbuf", [128, 4 * NC], "bfloat16"),
    "rtin": ("sbuf", [128, 4 * NC], "bfloat16"),
    "win": ("sbuf", [128, 4 * NC], "bfloat16"),
    "xc": ("sbuf", [128, NC], "float8_e4m3fn_x4"),
    "xs": ("sbuf", [128, NC], "uint8"),
    "rc": ("sbuf", [128, NC], "float8_e4m3fn_x4"),
    "rs": ("sbuf", [128, NC], "uint8"),
    "wc": ("sbuf", [128, N * NC], "float8_e4m3fn_x4"),
    "ws": ("sbuf", [128, N * NC], "uint8"),
    "top": ("sbuf", [128, 2], "float32"),
    "low": ("sbuf", [128, N], "float32"),
    "rest": ("sbuf", [128, N], "float32"),
    "take": ("sbuf", [128, N], "float32"),
    "gate": ("sbuf", [128, N], "float32"),
    "prod": ("sbuf", [128, N * NC], "float32"),
    "acc": ("sbuf", [128, NC], "float32"),
    "ps": ("psum", [128, BANK * (N + 1)], "float32"),
}
SEMAPHORES = (["wl", "xl", "rl", "wq", "xq", "rq", "ml", "v1", "v2", "v3", "v4", "v5", "gated", "stored", "sent", "hplane", "hcodes"]
              + ["arr%d" % e for e in range(N)] + ["mm%d" % e for e in range(N)] + ["pr%d" % e for e in range(N)]
              + ["ad%d" % k for k in range(1, N)])


def engines(mask):
    return bin(mask).count("1")


def routes(src, cores, topo):
    r = cores.index(src)
    around = [cores[(r + k) % len(cores)] for k in range(1, len(cores))]
    direct = [d for d in around if topo.may_write(src, d)]
    apart = [d for d in cores if d != src and not topo.may_write(src, d)]
    if not apart:
        return direct, []
    plane = [c for c in cores if c == src or topo.same_plane(c, src)]
    p = plane.index(src)
    owners = [c for c in range(CORES_ALL) if topo.host(c) == topo.host(src) and topo.chip(c) == topo.chip(src)
              and c not in cores and all(topo.may_write(c, d) for d in apart)]
    dies = sorted({topo.die(c) for c in owners})
    pools = [[c for c in owners if topo.die(c) == d] for d in dies]
    used = [0] * len(pools)
    first = p * len(apart) // len(plane)
    far = []
    for k in range(len(apart)):
        q = (first + k) % len(apart)
        i = (p + q) % len(pools)
        far.append((pools[i][used[i] % len(pools[i])], apart[q]))
        used[i] += 1
    return direct, far


def send(g, core, topo, dsts, mask, piece, arrival, done):
    ids = []
    for d in dsts:
        rid, pid = topo.addr(d, core)
        ids.append(DstId(rid=rid, pnc=pid))
    g.remote_dma_fused([RemoteDMATransfer(dst_ids=ids, dma_engine_mask=mask, remote_sem=arrival, srcs=[piece],
                                          dsts=[piece] * len(ids), alu_op=0)], local_sem=done)
    return engines(mask)


def codes_of(T, e):
    return T.wc[:, e * NC:(e + 1) * NC]


def plane_of(T, e):
    return T.ws[:, e * NC:(e + 1) * NC]


def handover_mask(core, relays, direct, topo):
    mask = topo.mask(core, relays[0])
    if len(relays) <= 2 and direct:
        mask &= ~topo.mask(core, direct[0])
    return mask


def relay_program(g, core, T, topo):
    cores = list(T.cores)
    for src in cores:
        if topo.host(src) != topo.host(core) or topo.chip(src) != topo.chip(core):
            continue
        direct, far = routes(src, cores, topo)
        dsts = [d for h, d in far if h == core]
        if not dsts:
            continue
        e = T.rank_of(src)
        n = engines(handover_mask(src, [h for h, d in far], direct, topo))
        arr = T.sem["arr%d" % e]
        mask = topo.mask(core, dsts[0])
        g.wait_ge(T.sem.hplane, n)
        sent = send(g, core, topo, dsts, mask, plane_of(T, e), arr, T.sem.sent)
        g.wait_ge(T.sem.hcodes, n)
        sent += send(g, core, topo, dsts, mask, codes_of(T, e).bitcast(dt.uint8), arr, T.sem.sent)
        g.wait_ge(T.sem.sent, sent)


def rank_program(g, core, T, topo):
    rank = T.rank_of(core)
    if rank is None:
        relay_program(g, core, T, topo)
        return
    S = T.sem
    cores = list(T.cores)
    direct, far = routes(core, cores, topo)

    for name, inp, sem in (("win", T.w, S.wl), ("xin", T.x, S.xl), ("rtin", T.rt, S.rl)):
        g.sync.dma_start(T[name][:], inp[:]).then_inc(sem, 16)

    for name, sem, codes, plane, out in (("win", S.wl, codes_of(T, rank), plane_of(T, rank), S.wq),
                                         ("xin", S.xl, T.xc[:], T.xs[:], S.xq), ("rtin", S.rl, T.rc[:], T.rs[:], S.rq)):
        g.vector.wait_ge(sem, 16)
        g.vector.quantize_mx(codes, plane, T[name][:]).then_inc(out, 1)

    mine = S["arr%d" % rank] if False else T.sem["arr%d" % rank]
    own_codes = codes_of(T, rank).bitcast(dt.uint8)
    sent = 0
    g.wait_ge(S.wq, 1)
    if far:
        relays = []
        for h, d in far:
            if h not in relays:
                relays.append(h)
        mask = handover_mask(core, relays, direct, topo)
        sent += send(g, core, topo, relays, mask, plane_of(T, rank), S.hplane, S.sent)
        sent += send(g, core, topo, relays, mask, own_codes, S.hcodes, S.sent)
    if direct:
        mask = topo.mask(core, direct[0])
        sent += send(g, core, topo, direct, mask, plane_of(T, rank), mine, S.sent)
        sent += send(g, core, topo, direct, mask, own_codes, mine, S.sent)
    g.wait_ge(S.sent, sent)

    order = []
    for src in cores:
        if src == core:
            continue
        d, f = routes(src, cores, topo)
        if core in d:
            order.append((0, d.index(core), T.rank_of(src), engines(topo.mask(src, core))))
        else:
            k = [x[1] for x in f].index(core)
            order.append((1, k, T.rank_of(src), engines(topo.mask(f[k][0], core))))
    order.sort()

    g.tensor.wait_ge(S.xq, 1)
    g.tensor.wait_ge(S.rq, 1)
    logits = N * BANK
    g.tensor.matmul_mx(T.ps[:, logits:logits + NC], T.xc[:], T.xs[:], T.rc[:], T.rs[:], True, True).then_inc(S.ml, 1)
    g.tensor.wait_ge(S.wq, 1)
    experts = [rank] + [o[2] for o in order]
    for k, e in enumerate(experts):
        if k:
            g.tensor.wait_ge(T.sem["arr%d" % e], 2 * order[k - 1][3])
        g.tensor.matmul_mx(T.ps[:, e * BANK:e * BANK + NC], T.xc[:], T.xs[:], codes_of(T, e), plane_of(T, e),
                           True, True).then_inc(T.sem["mm%d" % e], 1)

    L = T.ps[:, logits:logits + N]
    v = g.vector
    v.wait_ge(S.ml, 1)
    v.tensor_reduce(T.top[:, 0:1], L, AxisListType.X, AluOpType.max).then_inc(S.v1, 1)
    v.wait_ge(S.v1, 1)
    v.tensor_scalar(T.low[:], L, T.top[:, 0:1], -BIG, AluOpType.is_ge, AluOpType.mult).then_inc(S.v2, 1)
    v.wait_ge(S.v2, 1)
    v.tensor_tensor(T.rest[:], L, T.low[:], AluOpType.add).then_inc(S.v3, 1)
    v.wait_ge(S.v3, 1)
    v.tensor_reduce(T.top[:, 1:2], T.rest[:], AxisListType.X, AluOpType.max).then_inc(S.v4, 1)
    v.wait_ge(S.v4, 1)
    v.tensor_scalar(T.take[:], L, T.top[:, 1:2], None, AluOpType.is_ge).then_inc(S.v5, 1)
    v.wait_ge(S.v5, 1)
    v.tensor_tensor(T.gate[:], L, T.take[:], AluOpType.mult).then_inc(S.gated, 1)

    g.scalar.wait_ge(S.gated, 1)
    for e in experts:
        g.scalar.wait_ge(T.sem["mm%d" % e], 1)
        g.scalar.activation(T.prod[:, e * NC:(e + 1) * NC], T.ps[:, e * BANK:e * BANK + NC], ActivationFunctionType.Copy,
                            scale=T.gate[:, e:e + 1]).then_inc(T.sem["pr%d" % e], 1)
    e0 = experts[0]
    v.wait_ge(T.sem["pr%d" % e0], 1)
    for k in range(1, N):
        e = experts[k]
        v.wait_ge(T.sem["pr%d" % e], 1)
        if k == 1:
            before = T.prod[:, e0 * NC:(e0 + 1) * NC]
        else:
            v.wait_ge(T.sem["ad%d" % (k - 1)], 1)
            before = T.acc[:]
        v.tensor_tensor(T.acc[:], before, T.prod[:, e * NC:(e + 1) * NC], AluOpType.add).then_inc(T.sem["ad%d" % k], 1)

    g.sync.wait_ge(T.sem["ad%d" % (N - 1)], 1)
    g.sync.dma_start(T.y[:], T.acc[:]).then_inc(S.stored, 16)
    g.sync.wait_ge(S.stored, 16)
